import numpy as np
import ml_dtypes


def mxq(x, axis, fmt="e4m3"):
    dtype, down = {"e4m3": (ml_dtypes.float8_e4m3fn, 7), "e5m2": (ml_dtypes.float8_e5m2, 14)}[fmt]
    v = np.moveaxis(np.asarray(x, np.float32).astype(ml_dtypes.bfloat16).astype(np.float64), axis, -1)
    blocks = v.reshape(v.shape[:-1] + (-1, 32))
    amax = np.abs(blocks).max(-1, keepdims=True)
    byte = np.maximum(np.where(amax > 0, np.frexp(amax)[1] - 1 + 127, 0) - down, 1)
    scale = np.exp2(byte - 127.0)
    codes = (blocks / scale).astype(np.float32).astype(dtype).astype(np.float64)
    return np.moveaxis((codes * scale).reshape(v.shape), -1, axis)


WIDE = False


def mx_kscale(k):
    if not WIDE:
        return np.ones(k)
    levels = np.array([10, -10, 5, -5, 0])
    if k % 512:
        return np.exp2(np.random.permutation(np.resize(levels, k // 32))).repeat(32)
    a = np.empty((k // 512, 16))
    for p in range(k // 512):
        a[p, :8] = np.random.permutation(np.resize(levels, 8))
        for g in range(8):
            far = levels[np.abs(levels - a[p, g]) >= 10]
            a[p, g + 8] = far[np.random.randint(len(far))]
    return np.exp2(a.ravel()).repeat(32)


BF16 = ml_dtypes.bfloat16


def bf(x):
    return np.asarray(x, np.float32).astype(BF16)


def f64(x):
    return np.asarray(x).astype(np.float64)


E2M1 = np.array([0.0, 0.5, 1.0, 1.5, 2.0, 3.0, 4.0, 6.0, -0.0, -0.5, -1.0, -1.5, -2.0, -3.0, -4.0, -6.0])


def pack_weight(w, fmt):
    k, n = w.shape
    w = f64(bf(w)).reshape(k // 32, 32, n)
    amax = np.abs(w).max(1)
    if fmt == "e4m3":
        byte = np.frexp(amax)[1] - 1 + 127 - 7
    else:
        mant, ex = np.frexp(amax / 6.0)
        byte = np.where(mant > 0.5, ex, ex - 1) + 127
    byte = np.clip(np.where(amax > 0, byte, 1), 1, 254)
    scaled = (w * np.exp2(127.0 - byte)[:, None, :]).reshape(k, n).astype(np.float32)
    by_word = np.ascontiguousarray(scaled.reshape(k // 512, 128, 4, n).transpose(0, 1, 3, 2))
    if fmt == "e4m3":
        words = by_word.astype(ml_dtypes.float8_e4m3fn).view(np.uint8)
    else:
        c = by_word.astype(ml_dtypes.float4_e2m1fn).view(np.uint8) & 0xF
        words = c[..., 0::2] | (c[..., 1::2] << 4)
    return np.ascontiguousarray(words), np.ascontiguousarray(byte.astype(np.uint8).reshape(k // 512, 16, n))


def unpack_weight(words, scales, fmt):
    g, p, n, _ = words.shape
    if fmt == "e4m3":
        vals = np.ascontiguousarray(words).view(ml_dtypes.float8_e4m3fn).astype(np.float64)
    else:
        nib = np.empty((g, p, n, 4), np.uint8)
        nib[..., 0::2] = words & 0xF
        nib[..., 1::2] = words >> 4
        vals = E2M1[nib]
    vals = vals * np.repeat(np.exp2(scales.astype(np.float64) - 127.0), 8, axis=1)[..., None]
    return vals.transpose(0, 1, 3, 2).reshape(g * 512, n)
def pack4(w):
    words, scales = pack_weight(w, "e2m1")
    return words.reshape(words.shape[0], 128, -1), scales


def unpack4(words, scales):
    return unpack_weight(words.reshape(words.shape[0], 128, -1, 2), scales, "e2m1")


E4M3FN = np.array([(-1.0 if i & 128 else 1.0) * ((1.0 + (i & 7) / 8.0) * 2.0 ** (((i >> 3) & 15) - 7) if i & 120 else (i & 7) * 2.0 ** -9) for i in range(256)])


def e4m3fn_bytes(y):
    return np.clip(np.asarray(y, np.float64), -448.0, 448.0).astype(np.float32).astype(ml_dtypes.float8_e4m3fn).view(np.uint8)


def e4m3fn_values(b):
    return E4M3FN[b]


N, D, F = 512, 1024, 1024


def logistic(g):
    return 1.0 / (1.0 + np.exp(-g))


def draw0():
    s, t = mx_kscale(D), mx_kscale(F)
    x = bf(np.random.standard_normal((N, D)) * s)
    dx = bf(np.random.standard_normal((N, D)) * s)
    wg_words, wg_scales = pack4(np.random.standard_normal((D, F)) / np.sqrt(D) / s[:, None])
    wu_words, wu_scales = pack4(np.random.standard_normal((D, F)) / np.sqrt(D) / s[:, None] * t)
    wd_words, wd_scales = pack4(np.random.standard_normal((F, D)) / np.sqrt(F) / t[:, None])
    return {"x": x,
            "dx": dx,
            "wg_words": wg_words, "wg_scales": wg_scales,
            "wu_words": wu_words, "wu_scales": wu_scales,
            "wd_words": wd_words, "wd_scales": wd_scales}


def core(x, dx, wg_words, wg_scales, wu_words, wu_scales, wd_words, wd_scales):
    xq = mxq(f64(x), 1, "e4m3")
    dxq = mxq(f64(dx), 1, "e4m3")
    wgq = unpack4(wg_words, wg_scales)
    wuq = unpack4(wu_words, wu_scales)
    g = xq @ wgq
    dg = dxq @ wgq
    u = xq @ wuq
    du = dxq @ wuq
    s = logistic(g)
    sp = s * (1.0 + g * (1.0 - s))
    dh = sp * dg * u + g * s * du
    return mxq(dh, 1, "e4m3") @ unpack4(wd_words, wd_scales)


def setup_inputs():
    drawn = draw0()
    full = np.asarray(drawn['x']).astype(np.float64)
    scale = (np.abs(full).reshape(512, 8, 128).max(axis=(2,)) / 448.0).astype(np.float32)
    given = {}
    for key, value in drawn.items():
        if key == 'x':
            given['x_bytes'] = e4m3fn_bytes(full / np.repeat(scale.astype(np.float64), 128, axis=1))
            given['x_scale'] = scale
        else:
            given[key] = value
    return given


def reference(x_bytes, x_scale, dx, wg_words, wg_scales, wu_words, wu_scales, wd_words, wd_scales):
    return core(e4m3fn_values(x_bytes) * np.repeat(x_scale.astype(np.float64), 128, axis=1), dx, wg_words, wg_scales, wu_words, wu_scales, wd_words, wd_scales)

@@ -1,0 +1,429 @@
+from contextlib import ExitStack
+
+import concourse.mybir as mybir
+from concourse.masks import make_identity
+
+N, D, F = 512, 1024, 1024
+FLOPS = 5 * 2 * N * D * F
+
+P = 128
+TILES = N // P
+HALF = 512
+UNITS = 2 * TILES
+SPLIT_H = True
+
+F32 = mybir.dt.float32
+BF16 = mybir.dt.bfloat16
+I32 = mybir.dt.int32
+U32 = mybir.dt.uint32
+U8 = mybir.dt.uint8
+E4M3 = mybir.dt.float8_e4m3fn
+FP8X4 = mybir.dt.float8_e4m3fn_x4
+FP4X4 = mybir.dt.float4_e2m1fn_x4
+ALU = mybir.AluOpType
+ACT = mybir.ActivationFunctionType
+
+
+def tile_swigluforwardtangentjvp_d1p_kernel(
+    tc, x_bytes, x_scale, dx, wg_words, wg_scales, wu_words, wu_scales, wd_words, wd_scales, out
+):
+    nc = tc.nc
+    xb_v = x_bytes.rearrange("(p i) k -> p i k", i=TILES)
+    xs_v = x_scale.rearrange("(p i) j -> p i j", i=TILES)
+    dx_v = dx.rearrange("(p i) k -> p i k", i=TILES)
+    out_v = out.rearrange("(p i) d -> p i d", i=TILES)
+
+    with ExitStack() as ctx:
+        keep = ctx.enter_context(tc.tile_pool(name="keep", bufs=1))
+        work = ctx.enter_context(tc.tile_pool(name="work", bufs=3))
+        psum = ctx.enter_context(tc.psum_pool(name="psum", bufs=1))
+        ctx.enter_context(tc.manual_schedule())
+
+        ident = keep.tile([P, P], F32, name="ident")
+        xs = keep.tile([P, TILES, 8], F32, name="xs")
+        xb = keep.tile([P, TILES, D], U8, name="xb", align_bytes=64)
+        dxt = keep.tile([P, TILES, D], BF16, name="dxt", align_bytes=64)
+        one = keep.tile([P, 1], F32, name="one")
+        one_o = keep.tile([P, 1], F32, name="one_o")
+        words = {}
+        planes = {}
+        hbm = {"g": (wg_words, wg_scales), "u": (wu_words, wu_scales), "d": (wd_words, wd_scales)}
+        for w in "gud":
+            for h in range(2):
+                words[w, h] = keep.tile([P, 2, 1024], U8, name="words_%s%d" % (w, h), align_bytes=64)
+            planes[w] = keep.tile([P, 2, 1024], U8, name="plane_" + w, align_bytes=64)
+
+        def load_words(w, h):
+            nc.sync.dma_start(
+                out=words[w, h][:].bitcast(I32),
+                in_=hbm[w][0].bitcast(I32).rearrange("g p c -> p g c")[:, :, 256 * h : 256 * h + 256],
+            )
+
+        def load_scales(w, queue):
+            src = hbm[w][1].bitcast(I32)
+            dst = planes[w][:].bitcast(I32)
+            for q in range(4):
+                queue.dma_start(
+                    out=dst[32 * q : 32 * q + 4, :, :],
+                    in_=src[:, 4 * q : 4 * q + 4, :].rearrange("g r n -> r g n"),
+                )
+
+        def load_x(i):
+            nc.sync.dma_start(out=xb[:, i, :], in_=xb_v[:, i, :])
+
+        def load_dx(i):
+            nc.sync.dma_start(out=dxt[:, i, :], in_=dx_v[:, i, :])
+
+        nc.vector.memset(planes["g"][:].bitcast(I32), 0)
+        nc.vector.memset(one[:], 1.0)
+        nc.vector.memset(planes["u"][:].bitcast(I32), 0)
+        nc.vector.memset(planes["d"][:].bitcast(I32), 0)
+        make_identity(nc, ident[:])
+        nc.sync.dma_start(out=xs[:], in_=xs_v)
+        load_x(0)
+        load_dx(0)
+        load_scales("g", nc.scalar)
+        load_scales("u", nc.gpsimd)
+        nc.scalar.activation(out=one_o[:], in_=one[:], func=ACT.Silu)
+        load_words("g", 0)
+        load_words("u", 0)
+        load_x(1)
+        load_dx(1)
+        load_words("g", 1)
+        load_words("u", 1)
+        load_x(2)
+        load_dx(2)
+        load_words("d", 0)
+        load_words("d", 1)
+        load_scales("d", nc.gpsimd)
+        load_x(3)
+        load_dx(3)
+
+        xw = {}
+        bank = {}
+        grp = {}
+        codes = {}
+        scl = {}
+        val = {}
+        prod = {}
+
+        def widen(i, engines):
+            xw[i] = work.tile([P, D], BF16, name="xw%d" % i, tag="xw", align_bytes=64)
+            for b in range(8):
+                o = xw[i][:, 128 * b : 128 * b + 128]
+                v = xb[:, i, 128 * b : 128 * b + 128].bitcast(E4M3)
+                s = xs[:, i, b : b + 1]
+                if engines[b] == "V":
+                    nc.vector.tensor_scalar(out=o, in0=v, scalar1=s, scalar2=None, op0=ALU.mult)
+                else:
+                    nc.scalar.activation(out=o, in_=v, func=ACT.Copy, scale=s)
+
+        def widen_half(i, g, eng):
+            if i not in xw:
+                xw[i] = work.tile([P, D], BF16, name="xw%d" % i, tag="xw", align_bytes=64)
+            for b in range(4 * g, 4 * g + 4):
+                o = xw[i][:, 128 * b : 128 * b + 128]
+                v = xb[:, i, 128 * b : 128 * b + 128].bitcast(E4M3)
+                s = xs[:, i, b : b + 1]
+                if eng == "V":
+                    nc.vector.tensor_scalar(out=o, in0=v, scalar1=s, scalar2=None, op0=ALU.mult)
+                else:
+                    nc.scalar.activation(out=o, in_=v, func=ACT.Copy, scale=s)
+
+        def turn_xp(i, g, tag="aux"):
+            turn("x%d" % i, [(g, xw[i][:, 512 * g : 512 * g + 512])], tag)
+
+        def turn_dxp(i, g, tag="aux"):
+            turn("dx%d" % i, [(g, dxt[:, i, 512 * g : 512 * g + 512])], tag)
+
+        def copy(eng, out, in_):
+            if eng == "V":
+                nc.vector.tensor_copy(out=out, in_=in_)
+            else:
+                nc.scalar.copy(out=out, in_=in_)
+
+        def turn(key, parts, tag="aux"):
+            t = psum.tile([P, 4, P], F32, name="turn_%s_%d" % (key, parts[0][0]), tag=tag, bufs=3 if tag == "aux" else 1)
+            for g, part in parts:
+                w = part.bitcast(F32)
+                for u in range(2):
+                    cols = slice(128 * u, 128 * u + 128) if SPLIT_H and key[0] == "h" else slice(u, 256, 2)
+                    nc.tensor.transpose(t[:, 2 * g + u, :], w[:, cols], ident[:])
+                bank[key, g] = t
+
+        def turn_x(i):
+            turn("x%d" % i, [(g, xw[i][:, 512 * g : 512 * g + 512]) for g in range(2)])
+
+        def turn_dx(i):
+            turn("dx%d" % i, [(g, dxt[:, i, 512 * g : 512 * g + 512]) for g in range(2)])
+
+        def turn_h(i, halves=(0, 1)):
+            turn("h%d" % i, [(g, val["dh", 2 * i + g][:]) for g in halves])
+
+        def lift(key, eng, passes=(0, 1)):
+            if key not in grp:
+                grp[key] = work.tile([P, 2, P, 4], BF16, name="grp_" + key, tag="grp", bufs=5, align_bytes=64)
+            g0, g1 = passes[0], passes[-1] + 1
+            o = grp[key][:].rearrange("p g r t -> p (g r t)").bitcast(F32).rearrange("p (g r u) -> p g r u", g=2, u=2)
+            v = bank[key, g0][:].rearrange("p (g u) r -> p g r u", u=2)
+            copy(eng, o[:, g0:g1, :, :], v[:, g0:g1, :, :])
+
+        def quant(key, passes=(0, 1)):
+            if key not in codes:
+                codes[key] = work.tile([P, 2, P], U32, name="codes_" + key, tag="codes", bufs=8, align_bytes=64)
+                scl[key] = work.tile([P, 2, P], U8, name="scl_" + key, tag="scl", bufs=8, align_bytes=64)
+            g0, g1 = passes[0], passes[-1] + 1
+            nc.vector.quantize_mx(
+                out=codes[key][:, g0:g1, :].rearrange("p g r -> p (g r)").bitcast(FP8X4),
+                scales=scl[key][:, g0:g1, :].rearrange("p g r -> p (g r)"),
+                in_=grp[key][:, g0:g1, :, :].rearrange("p g r t -> p (g r t)"),
+            )
+
+        def passes_into(t, key, w, h, passes=(0, 1)):
+            for g in passes:
+                nc.tensor.matmul_mx(
+                    out=t[:],
+                    lhsT=codes[key][:, g, :].bitcast(FP8X4),
+                    lhsT_scale=scl[key][:, g, :],
+                    rhs=words[w, h][:, g, :].bitcast(FP4X4),
+                    rhs_scale=planes[w][:, g, HALF * h : HALF * h + HALF],
+                    start=(g == 0),
+                    stop=(g == 1),
+                )
+
+        def product(kind, j):
+            if j >= UNITS:
+                return
+            i, h = divmod(j, 2)
+            t = psum.tile([P, HALF], F32, name="%s_%d" % (kind, j), tag="bank_" + kind, bufs=2 if kind == "g" else 1)
+            passes_into(t, ("dx%d" if kind[0] == "d" else "x%d") % i, kind[-1], h)
+            prod[kind, j] = t
+
+        def act(name, j):
+            if j >= UNITS:
+                return
+            func, scale = {"b": (ACT.Silu, -1.0), "th": (ACT.Tanh, 0.5), "a": (ACT.Silu, 1.0)}[name]
+            t = work.tile([P, HALF], F32, name="%s_%d" % (name, j), tag=name)
+            nc.scalar.activation(out=t[:], in_=prod["g", j][:], func=func, scale=scale)
+            val[name, j] = t
+
+        def fresh(name, j, dt=F32):
+            t = work.tile([P, HALF], dt, name="%s_%d" % (name, j), tag=name, align_bytes=64)
+            val[name, j] = t
+            return t
+
+        def m1(j):
+            t = fresh("m1", j)
+            nc.vector.scalar_tensor_tensor(
+                out=t[:], in0=val["b", j][:], scalar=1.0, in1=prod["dg", j][:], op0=ALU.subtract, op1=ALU.mult
+            )
+
+        def m2(j):
+            t = fresh("m2", j)
+            nc.vector.scalar_tensor_tensor(
+                out=t[:], in0=val["th", j][:], scalar=1.0, in1=prod["u", j][:], op0=ALU.add, op1=ALU.mult
+            )
+
+        def m3(j):
+            t = fresh("m3", j)
+            nc.vector.scalar_tensor_tensor(
+                out=t[:], in0=val["a", j][:], scalar=-2.0, in1=prod["du", j][:], op0=ALU.mult, op1=ALU.mult
+            )
+
+        def m4(j, eng="V"):
+            t = fresh("m4", j)
+            e = nc.vector if eng == "V" else nc.gpsimd
+            e.tensor_tensor(out=t[:], in0=val["m1", j][:], in1=val["m2", j][:], op=ALU.mult)
+
+        def dh(j, eng="V"):
+            if j < 0:
+                return
+            t = fresh("dh", j, BF16)
+            e = nc.vector if eng == "V" else nc.gpsimd
+            o, a, b = t[:], val["m3", j][:], val["m4", j][:]
+            if SPLIT_H:
+                o = o.rearrange("p (u q e) -> p q u e", u=2, e=2)
+                a = a.rearrange("p (q u e) -> p q u e", u=2, e=2)
+                b = b.rearrange("p (q u e) -> p q u e", u=2, e=2)
+            e.tensor_tensor(out=o, in0=a, in1=b, op=ALU.add)
+
+        def down(i, n, passes=(0, 1)):
+            if ("o", i, n) not in prod:
+                prod["o", i, n] = psum.tile([P, HALF], F32, name="down_%d_%d" % (i, n), tag="aux", bufs=3)
+            passes_into(prod["o", i, n], "h%d" % i, "d", n, passes)
+
+        def store(i, n, eng, queue=None):
+            t = work.tile([P, HALF], F32, name="out_%d_%d" % (i, n), tag="out", bufs=4)
+            if eng == "V":
+                nc.vector.tensor_scalar(out=t[:], in0=prod["o", i, n][:], scalar1=-0.5, scalar2=None, op0=ALU.mult)
+            else:
+                nc.scalar.activation(out=t[:], in_=prod["o", i, n][:], func=ACT.Copy, scale=-0.5)
+            (queue or nc.sync).dma_start(out=out_v[:, i, HALF * n : HALF * n + HALF], in_=t[:])
+
+        widen_half(0, 1, "V")
+        turn_xp(0, 1)
+        turn_dxp(0, 0, "bank_u")
+        lift("dx0", "V", (0,))
+        widen_half(0, 0, "S")
+        turn_xp(0, 0)
+        lift("x0", "S", (1,))
+        lift("x0", "V", (0,))
+        quant("dx0", (0,))
+        quant("x0", (0,))
+        turn_dxp(0, 1, "bank_du")
+        lift("dx0", "S", (1,))
+        quant("dx0", (1,))
+        widen_half(1, 1, "S")
+        quant("x0", (1,))
+        widen_half(1, 0, "V")
+        product("g", 0)
+        turn_dx(1)
+        turn_x(1)
+        lift("dx1", "V")
+        product("g", 1)
+        act("th", 0)
+        product("u", 0)
+        act("b", 0)
+        act("a", 0)
+        product("dg", 0)
+        product("du", 0)
+        lift("x1", "V")
+        quant("dx1")
+        quant("x1")
+        act("th", 1)
+        m2(0)
+        m1(0)
+        m3(0)
+        m4(0, "V")
+        product("u", 1)
+        turn_dx(2)
+        m2(1)
+        widen_half(2, 1, "S")
+        act("b", 1)
+        act("a", 1)
+        product("dg", 1)
+        lift("dx2", "S")
+        product("du", 1)
+        dh(0, "V")
+        product("g", 2)
+        m1(1)
+        widen_half(2, 0, "S")
+        m3(1)
+        m4(1, "V")
+        product("g", 3)
+        act("th", 2)
+        product("u", 2)
+        act("b", 2)
+        act("a", 2)
+        product("dg", 2)
+        product("du", 2)
+        turn_x(2)
+        quant("dx2")
+        act("th", 3)
+        m2(2)
+        dh(1, "V")
+        m1(2)
+        m3(2)
+        m4(2, "V")
+        product("u", 3)
+        turn_dx(3)
+        m2(3)
+        turn_h(0)
+        widen_half(3, 1, "S")
+        act("b", 3)
+        lift("x2", "S")
+        act("a", 3)
+        product("dg", 3)
+        lift("dx3", "S")
+        product("du", 3)
+        quant("x2")
+        dh(2, "V")
+        product("g", 4)
+        m1(3)
+        widen_half(3, 0, "S")
+        lift("h0", "S")
+        m3(3)
+        m4(3, "V")
+        product("g", 5)
+        act("th", 4)
+        product("u", 4)
+        quant("h0")
+        act("b", 4)
+        act("a", 4)
+        product("dg", 4)
+        product("du", 4)
+        turn_x(3)
+        quant("dx3")
+        act("th", 5)
+        m2(4)
+        dh(3, "V")
+        m1(4)
+        m3(4)
+        m4(4, "V")
+        product("u", 5)
+        m2(5)
+        turn_h(1)
+        act("b", 5)
+        lift("x3", "S")
+        act("a", 5)
+        product("dg", 5)
+        product("du", 5)
+        quant("x3")
+        dh(4, "V")
+        product("g", 6)
+        m1(5)
+        lift("h1", "S")
+        m3(5)
+        m4(5, "V")
+        product("g", 7)
+        act("th", 6)
+        product("u", 6)
+        quant("h1")
+        act("b", 6)
+        act("a", 6)
+        product("dg", 6)
+        product("du", 6)
+        down(0, 1)
+        act("th", 7)
+        m2(6)
+        dh(5, "V")
+        m1(6)
+        m3(6)
+        product("u", 7)
+        m2(7)
+        turn_h(2)
+        act("b", 7)
+        store(0, 1, "S")
+        m4(6, "V")
+        act("a", 7)
+        product("dg", 7)
+        product("du", 7)
+        m1(7)
+        lift("h2", "S")
+        m3(7)
+        down(0, 0)
+        quant("h2")
+        down(1, 1)
+        store(0, 0, "S")
+        m4(7, "V")
+        store(1, 1, "S")
+        dh(6, "V")
+        down(1, 0)
+        dh(7, "V")
+        down(2, 1)
+        turn_h(3, (0,))
+        store(1, 0, "S")
+        turn_h(3, (1,))
+        lift("h3", "V", (0,))
+        store(2, 1, "S")
+        quant("h3", (0,))
+        lift("h3", "S", (1,))
+        down(2, 0)
+        down(3, 1, (0,))
+        store(2, 0, "S")
+        quant("h3", (1,))
+        down(3, 1, (1,))
+        store(3, 1, "S")
+        down(3, 0, (0,))
+        down(3, 0, (1,))
+        store(3, 0, "V")

@@ -59,10 +59,10 @@ def tile_swigluforwardtangentjvp_d1p_kernel(
                 in_=hbm[w][0].bitcast(I32).rearrange("g p c -> p g c")[:, :, 256 * h : 256 * h + 256],
             )
 
-        def load_scales(w, queue):
+        def load_scales(w, queue, quadrants=range(4)):
             src = hbm[w][1].bitcast(I32)
             dst = planes[w][:].bitcast(I32)
-            for q in range(4):
+            for q in quadrants:
                 queue.dma_start(
                     out=dst[32 * q : 32 * q + 4, :, :],
                     in_=src[:, 4 * q : 4 * q + 4, :].rearrange("g r n -> r g n"),
@@ -83,9 +83,10 @@ def tile_swigluforwardtangentjvp_d1p_kernel(
         load_x(0)
         load_dx(0)
         load_scales("g", nc.scalar)
-        load_scales("u", nc.gpsimd)
+        load_scales("u", nc.gpsimd, (0, 1))
         nc.scalar.activation(out=one_o[:], in_=one[:], func=ACT.Silu)
         load_words("g", 0)
+        load_scales("u", nc.scalar, (2, 3))
         load_words("u", 0)
         load_x(1)
         load_dx(1)
@@ -252,6 +253,16 @@ def tile_swigluforwardtangentjvp_d1p_kernel(
                 prod["o", i, n] = psum.tile([P, HALF], F32, name="down_%d_%d" % (i, n), tag="aux", bufs=3)
             passes_into(prod["o", i, n], "h%d" % i, "d", n, passes)
 
+        def store_half(i, n, c, eng):
+            t = work.tile([P, 256], F32, name="out_%d_%d_%d" % (i, n, c), tag="outh", bufs=4)
+            src = prod["o", i, n][:, 256 * c : 256 * c + 256]
+            if eng == "V":
+                nc.vector.tensor_scalar(out=t[:], in0=src, scalar1=-0.5, scalar2=None, op0=ALU.mult)
+            else:
+                nc.scalar.activation(out=t[:], in_=src, func=ACT.Copy, scale=-0.5)
+            lo = HALF * n + 256 * c
+            (nc.sync if eng == "V" else nc.scalar).dma_start(out=out_v[:, i, lo : lo + 256], in_=t[:])
+
         def store(i, n, eng, queue=None):
             t = work.tile([P, HALF], F32, name="out_%d_%d" % (i, n), tag="out", bufs=4)
             if eng == "V":
@@ -260,170 +271,172 @@ def tile_swigluforwardtangentjvp_d1p_kernel(
                 nc.scalar.activation(out=t[:], in_=prod["o", i, n][:], func=ACT.Copy, scale=-0.5)
             (queue or nc.sync).dma_start(out=out_v[:, i, HALF * n : HALF * n + HALF], in_=t[:])
 
-        widen_half(0, 1, "V")
+        widen_half(0, 0, "V")
+        widen_half(0, 1, "S")
+        turn_xp(0, 0)
         turn_xp(0, 1)
         turn_dxp(0, 0, "bank_u")
-        lift("dx0", "V", (0,))
-        widen_half(0, 0, "S")
-        turn_xp(0, 0)
-        lift("x0", "S", (1,))
         lift("x0", "V", (0,))
-        quant("dx0", (0,))
-        quant("x0", (0,))
         turn_dxp(0, 1, "bank_du")
+        quant("x0", (0,))
+        lift("x0", "S", (1,))
+        lift("dx0", "S", (0,))
         lift("dx0", "S", (1,))
-        quant("dx0", (1,))
-        widen_half(1, 1, "S")
         quant("x0", (1,))
-        widen_half(1, 0, "V")
+        widen_half(1, 1, "V")
+        quant("dx0", (0,))
+        quant("dx0", (1,))
+        widen_half(1, 0, "S")
         product("g", 0)
-        turn_dx(1)
-        turn_x(1)
-        lift("dx1", "V")
-        product("g", 1)
         act("th", 0)
         product("u", 0)
         act("b", 0)
         act("a", 0)
+        turn_dx(1)
+        turn_x(1)
         product("dg", 0)
-        product("du", 0)
-        lift("x1", "V")
-        quant("dx1")
-        quant("x1")
-        act("th", 1)
+        product("g", 1)
         m2(0)
-        m1(0)
-        m3(0)
-        m4(0, "V")
+        lift("dx1", "V")
+        product("du", 0)
         product("u", 1)
-        turn_dx(2)
-        m2(1)
-        widen_half(2, 1, "S")
-        act("b", 1)
+        lift("x1", "S")
         act("a", 1)
-        product("dg", 1)
-        lift("dx2", "S")
-        product("du", 1)
-        dh(0, "V")
+        quant("dx1")
+        m1(0)
+        act("th", 1)
+        act("b", 1)
+        quant("x1")
         product("g", 2)
-        m1(1)
+        widen_half(2, 1, "S")
+        m4(0, "V")
+        product("dg", 1)
+        m3(0)
+        product("du", 1)
         widen_half(2, 0, "S")
+        act("th", 2)
+        m2(1)
+        product("u", 2)
+        dh(0, "V")
+        act("b", 2)
+        turn_x(2)
+        m1(1)
+        act("a", 2)
         m3(1)
         m4(1, "V")
-        product("g", 3)
-        act("th", 2)
-        product("u", 2)
-        act("b", 2)
-        act("a", 2)
         product("dg", 2)
-        product("du", 2)
-        turn_x(2)
-        quant("dx2")
-        act("th", 3)
+        product("g", 3)
         m2(2)
-        dh(1, "V")
-        m1(2)
-        m3(2)
-        m4(2, "V")
-        product("u", 3)
-        turn_dx(3)
-        m2(3)
-        turn_h(0)
-        widen_half(3, 1, "S")
-        act("b", 3)
         lift("x2", "S")
+        product("du", 2)
+        product("u", 3)
         act("a", 3)
-        product("dg", 3)
-        lift("dx3", "S")
-        product("du", 3)
+        m1(2)
+        act("th", 3)
+        turn_dx(2)
+        act("b", 3)
+        dh(1, "V")
+        turn_h(0)
         quant("x2")
-        dh(2, "V")
         product("g", 4)
-        m1(3)
+        widen_half(3, 1, "S")
+        lift("dx2", "S")
+        m4(2, "V")
+        product("dg", 3)
+        m3(2)
+        product("du", 3)
         widen_half(3, 0, "S")
+        act("th", 4)
         lift("h0", "S")
+        m2(3)
+        product("u", 4)
+        dh(2, "V")
+        act("b", 4)
+        quant("dx2")
+        turn_x(3)
+        m1(3)
+        act("a", 4)
         m3(3)
         m4(3, "V")
-        product("g", 5)
-        act("th", 4)
-        product("u", 4)
-        quant("h0")
-        act("b", 4)
-        act("a", 4)
         product("dg", 4)
-        product("du", 4)
-        turn_x(3)
-        quant("dx3")
-        act("th", 5)
+        product("g", 5)
         m2(4)
-        dh(3, "V")
-        m1(4)
-        m3(4)
-        m4(4, "V")
-        product("u", 5)
-        m2(5)
-        turn_h(1)
-        act("b", 5)
+        quant("h0")
         lift("x3", "S")
+        product("du", 4)
+        product("u", 5)
         act("a", 5)
-        product("dg", 5)
-        product("du", 5)
+        m1(4)
+        act("th", 5)
+        turn_dx(3)
+        act("b", 5)
+        dh(3, "V")
+        turn_h(1)
         quant("x3")
-        dh(4, "V")
         product("g", 6)
-        m1(5)
+        lift("dx3", "S")
+        m4(4, "V")
+        product("dg", 5)
+        m3(4)
+        product("du", 5)
+        act("th", 6)
         lift("h1", "S")
+        m2(5)
+        product("u", 6)
+        dh(4, "V")
+        act("b", 6)
+        quant("dx3")
+        m1(5)
+        act("a", 6)
         m3(5)
         m4(5, "V")
-        product("g", 7)
-        act("th", 6)
-        product("u", 6)
-        quant("h1")
-        act("b", 6)
-        act("a", 6)
         product("dg", 6)
-        product("du", 6)
-        down(0, 1)
-        act("th", 7)
+        product("g", 7)
         m2(6)
-        dh(5, "V")
-        m1(6)
-        m3(6)
+        quant("h1")
+        product("du", 6)
         product("u", 7)
-        m2(7)
-        turn_h(2)
-        act("b", 7)
-        store(0, 1, "S")
-        m4(6, "V")
         act("a", 7)
+        m1(6)
+        act("th", 7)
+        act("b", 7)
+        dh(5, "V")
+        down(0, 1)
+        turn_h(2)
+        store(0, 1, "S")
         product("dg", 7)
+        m3(6)
         product("du", 7)
-        m1(7)
         lift("h2", "S")
+        m2(7)
+        m4(6, "V")
+        m1(7)
         m3(7)
-        down(0, 0)
         quant("h2")
-        down(1, 1)
-        store(0, 0, "S")
+        down(0, 0)
         m4(7, "V")
+        store(0, 0, "S")
+        down(1, 1)
         store(1, 1, "S")
-        dh(6, "V")
         down(1, 0)
-        dh(7, "V")
-        down(2, 1)
-        turn_h(3, (0,))
         store(1, 0, "S")
-        turn_h(3, (1,))
-        lift("h3", "V", (0,))
+        dh(6, "V")
+        down(2, 1)
         store(2, 1, "S")
-        quant("h3", (0,))
+        dh(7, "V")
+        turn_h(3, (0,))
+        turn_h(3, (1,))
+        lift("h3", "S", (0,))
         lift("h3", "S", (1,))
         down(2, 0)
-        down(3, 1, (0,))
         store(2, 0, "S")
-        quant("h3", (1,))
-        down(3, 1, (1,))
-        store(3, 1, "S")
+        quant("h3", (0,))
         down(3, 0, (0,))
+        down(3, 1, (0,))
+        quant("h3", (1,))
         down(3, 0, (1,))
-        store(3, 0, "V")
+        down(3, 1, (1,))
+        store_half(3, 0, 0, "S")
+        store_half(3, 0, 1, "V")
+        store_half(3, 1, 0, "V")
+        store_half(3, 1, 1, "S")

@@ -10,7 +10,7 @@ P = 128
 TILES = N // P
 HALF = 512
 UNITS = 2 * TILES
-SPLIT_H = True
+SPLIT_H = False
 
 F32 = mybir.dt.float32
 BF16 = mybir.dt.bfloat16
@@ -79,14 +79,13 @@ def tile_swigluforwardtangentjvp_d1p_kernel(
         nc.vector.memset(planes["u"][:].bitcast(I32), 0)
         nc.vector.memset(planes["d"][:].bitcast(I32), 0)
         make_identity(nc, ident[:])
-        nc.sync.dma_start(out=xs[:], in_=xs_v)
+        nc.scalar.dma_start(out=xs[:], in_=xs_v)
         load_x(0)
         load_dx(0)
-        load_scales("g", nc.scalar)
-        load_scales("u", nc.gpsimd, (0, 1))
+        load_scales("g", nc.sync)
+        load_scales("u", nc.gpsimd)
         nc.scalar.activation(out=one_o[:], in_=one[:], func=ACT.Silu)
         load_words("g", 0)
-        load_scales("u", nc.scalar, (2, 3))
         load_words("u", 0)
         load_x(1)
         load_dx(1)
@@ -264,7 +263,7 @@ def tile_swigluforwardtangentjvp_d1p_kernel(
             (nc.sync if eng == "V" else nc.scalar).dma_start(out=out_v[:, i, lo : lo + 256], in_=t[:])
 
         def store(i, n, eng, queue=None):
-            t = work.tile([P, HALF], F32, name="out_%d_%d" % (i, n), tag="out", bufs=4)
+            t = work.tile([P, HALF], F32, name="out_%d_%d" % (i, n), tag="out", bufs=8)
             if eng == "V":
                 nc.vector.tensor_scalar(out=t[:], in0=prod["o", i, n][:], scalar1=-0.5, scalar2=None, op0=ALU.mult)
             else:
@@ -272,171 +271,169 @@ def tile_swigluforwardtangentjvp_d1p_kernel(
             (queue or nc.sync).dma_start(out=out_v[:, i, HALF * n : HALF * n + HALF], in_=t[:])
 
         widen_half(0, 0, "V")
-        widen_half(0, 1, "S")
         turn_xp(0, 0)
+        lift("x0", "V", (0,))
+        widen_half(0, 1, "S")
+        quant("x0", (0,))
         turn_xp(0, 1)
         turn_dxp(0, 0, "bank_u")
-        lift("x0", "V", (0,))
         turn_dxp(0, 1, "bank_du")
-        quant("x0", (0,))
         lift("x0", "S", (1,))
-        lift("dx0", "S", (0,))
-        lift("dx0", "S", (1,))
         quant("x0", (1,))
-        widen_half(1, 1, "V")
+        lift("dx0", "V", (0,))
+        lift("dx0", "V", (1,))
         quant("dx0", (0,))
         quant("dx0", (1,))
-        widen_half(1, 0, "S")
+        widen_half(1, 1, "S")
+        widen_half(1, 0, "V")
         product("g", 0)
-        act("th", 0)
-        product("u", 0)
-        act("b", 0)
-        act("a", 0)
-        turn_dx(1)
-        turn_x(1)
         product("dg", 0)
+        turn_x(1)
+        turn_dx(1)
+        lift("x1", "V")
+        act("b", 0)
+        act("th", 0)
         product("g", 1)
-        m2(0)
-        lift("dx1", "V")
-        product("du", 0)
-        product("u", 1)
-        lift("x1", "S")
-        act("a", 1)
-        quant("dx1")
-        m1(0)
-        act("th", 1)
-        act("b", 1)
+        act("a", 0)
         quant("x1")
-        product("g", 2)
-        widen_half(2, 1, "S")
-        m4(0, "V")
+        product("u", 0)
+        lift("dx1", "S")
+        m1(0)
+        product("du", 0)
         product("dg", 1)
+        act("b", 1)
+        m2(0)
+        quant("dx1")
+        act("a", 1)
         m3(0)
+        m1(1)
+        product("u", 1)
+        product("g", 2)
+        act("th", 1)
+        m4(0, "V")
         product("du", 1)
         widen_half(2, 0, "S")
-        act("th", 2)
         m2(1)
-        product("u", 2)
-        dh(0, "V")
-        act("b", 2)
-        turn_x(2)
-        m1(1)
-        act("a", 2)
-        m3(1)
-        m4(1, "V")
         product("dg", 2)
+        widen_half(2, 1, "S")
+        act("b", 2)
+        dh(0, "V")
+        m4(1, "V")
+        act("th", 2)
         product("g", 3)
-        m2(2)
+        act("a", 2)
+        product("u", 2)
+        turn_x(2)
         lift("x2", "S")
-        product("du", 2)
-        product("u", 3)
-        act("a", 3)
-        m1(2)
-        act("th", 3)
         turn_dx(2)
-        act("b", 3)
-        dh(1, "V")
-        turn_h(0)
-        quant("x2")
-        product("g", 4)
-        widen_half(3, 1, "S")
-        lift("dx2", "S")
-        m4(2, "V")
+        m3(1)
+        m1(2)
+        product("du", 2)
         product("dg", 3)
+        dh(1, "V")
+        act("b", 3)
+        m2(2)
+        quant("x2")
+        lift("dx2", "S")
+        turn_h(0)
+        act("a", 3)
         m3(2)
+        m1(3)
+        product("u", 3)
+        product("g", 4)
+        act("th", 3)
+        quant("dx2")
+        lift("h0", "S")
+        m4(2, "V")
         product("du", 3)
         widen_half(3, 0, "S")
-        act("th", 4)
-        lift("h0", "S")
         m2(3)
-        product("u", 4)
-        dh(2, "V")
-        act("b", 4)
-        quant("dx2")
-        turn_x(3)
-        m1(3)
-        act("a", 4)
-        m3(3)
-        m4(3, "V")
         product("dg", 4)
-        product("g", 5)
-        m2(4)
         quant("h0")
+        widen_half(3, 1, "S")
+        act("b", 4)
+        dh(2, "V")
+        m4(3, "V")
+        act("th", 4)
+        product("g", 5)
+        act("a", 4)
+        product("u", 4)
+        turn_x(3)
         lift("x3", "S")
-        product("du", 4)
-        product("u", 5)
-        act("a", 5)
-        m1(4)
-        act("th", 5)
         turn_dx(3)
-        act("b", 5)
-        dh(3, "V")
-        turn_h(1)
-        quant("x3")
-        product("g", 6)
-        lift("dx3", "S")
-        m4(4, "V")
+        m3(3)
+        m1(4)
+        product("du", 4)
         product("dg", 5)
+        dh(3, "V")
+        act("b", 5)
+        m2(4)
+        quant("x3")
+        lift("dx3", "S")
+        turn_h(1)
+        act("a", 5)
         m3(4)
-        product("du", 5)
-        act("th", 6)
-        lift("h1", "S")
-        m2(5)
-        product("u", 6)
-        dh(4, "V")
-        act("b", 6)
-        quant("dx3")
         m1(5)
-        act("a", 6)
-        m3(5)
-        m4(5, "V")
-        product("dg", 6)
-        product("g", 7)
-        m2(6)
-        quant("h1")
-        product("du", 6)
-        product("u", 7)
-        act("a", 7)
-        m1(6)
-        act("th", 7)
-        act("b", 7)
-        dh(5, "V")
+        product("u", 5)
+        product("g", 6)
+        act("th", 5)
         down(0, 1)
-        turn_h(2)
-        store(0, 1, "S")
+        quant("dx3")
+        lift("h1", "S")
+        m4(4, "V")
+        product("du", 5)
+        m2(5)
+        product("dg", 6)
+        quant("h1")
+        act("b", 6)
+        dh(4, "V")
+        m4(5, "V")
+        act("th", 6)
+        product("g", 7)
+        act("a", 6)
+        product("u", 6)
+        m3(5)
+        m1(6)
+        product("du", 6)
         product("dg", 7)
+        dh(5, "V")
+        act("b", 7)
+        m2(6)
+        turn_h(2)
+        act("a", 7)
         m3(6)
-        product("du", 7)
-        lift("h2", "S")
-        m2(7)
-        m4(6, "V")
         m1(7)
-        m3(7)
-        quant("h2")
-        down(0, 0)
-        m4(7, "V")
-        store(0, 0, "S")
+        product("u", 7)
+        act("th", 7)
         down(1, 1)
-        store(1, 1, "S")
-        down(1, 0)
-        store(1, 0, "S")
-        dh(6, "V")
+        lift("h2", "S")
+        product("du", 7)
+        m4(6, "V")
+        m2(7)
+        quant("h2")
+        m4(7, "V")
+        store(0, 1, "S")
+        m3(7)
+        down(0, 0)
         down(2, 1)
-        store(2, 1, "S")
+        dh(6, "V")
+        store(1, 1, "S")
         dh(7, "V")
+        store(0, 0, "S")
+        down(1, 0)
         turn_h(3, (0,))
+        store(2, 1, "S")
+        store(1, 0, "S")
         turn_h(3, (1,))
         lift("h3", "S", (0,))
-        lift("h3", "S", (1,))
         down(2, 0)
+        lift("h3", "S", (1,))
         store(2, 0, "S")
         quant("h3", (0,))
         down(3, 0, (0,))
-        down(3, 1, (0,))
         quant("h3", (1,))
+        down(3, 1, (0,))
         down(3, 0, (1,))
         down(3, 1, (1,))
-        store_half(3, 0, 0, "S")
-        store_half(3, 0, 1, "V")
-        store_half(3, 1, 0, "V")
-        store_half(3, 1, 1, "S")
+        store(3, 0, "S")
+        store(3, 1, "V")

@@ -83,21 +83,18 @@ def tile_swigluforwardtangentjvp_d1p_kernel(
         load_x(0)
         load_dx(0)
         load_scales("g", nc.sync)
-        load_scales("u", nc.gpsimd)
         nc.scalar.activation(out=one_o[:], in_=one[:], func=ACT.Silu)
         load_words("g", 0)
+        load_scales("u", nc.sync)
         load_words("u", 0)
-        load_x(1)
+        nc.sync.dma_start(out=xb[:, 1:4, :], in_=xb_v[:, 1:4, :])
         load_dx(1)
         load_words("g", 1)
         load_words("u", 1)
-        load_x(2)
-        load_dx(2)
+        nc.sync.dma_start(out=dxt[:, 2:4, :], in_=dx_v[:, 2:4, :])
         load_words("d", 0)
         load_words("d", 1)
-        load_scales("d", nc.gpsimd)
-        load_x(3)
-        load_dx(3)
+        load_scales("d", nc.sync)
 
         xw = {}
         bank = {}
@@ -158,33 +155,52 @@ def tile_swigluforwardtangentjvp_d1p_kernel(
             turn("dx%d" % i, [(g, dxt[:, i, 512 * g : 512 * g + 512]) for g in range(2)])
 
         def turn_h(i, halves=(0, 1)):
-            turn("h%d" % i, [(g, val["dh", 2 * i + g][:]) for g in halves])
+            turn("h%d" % i, [(g, half("dh", 2 * i + g, BF16)) for g in halves])
+
+        def place(store, key, shape, dtype, tag, bufs):
+            if key[0] == "h":
+                if key not in store:
+                    store[key] = work.tile([P] + shape, dtype, name=tag + key, tag=tag + "h", bufs=bufs, align_bytes=64)
+                return store[key][:]
+            i = key[-1]
+            if "xd" + i not in store:
+                store["xd" + i] = work.tile([P, 2] + shape, dtype, name=tag + "xd" + i, tag=tag, bufs=bufs, align_bytes=64)
+            return store["xd" + i][:, 1 if key[0] == "d" else 0]
 
         def lift(key, eng, passes=(0, 1)):
-            if key not in grp:
-                grp[key] = work.tile([P, 2, P, 4], BF16, name="grp_" + key, tag="grp", bufs=5, align_bytes=64)
+            t = place(grp, key, [2, P, 4], BF16, "grp", 3)
             g0, g1 = passes[0], passes[-1] + 1
-            o = grp[key][:].rearrange("p g r t -> p (g r t)").bitcast(F32).rearrange("p (g r u) -> p g r u", g=2, u=2)
+            o = t.rearrange("p g r t -> p (g r t)").bitcast(F32).rearrange("p (g r u) -> p g r u", g=2, u=2)
             v = bank[key, g0][:].rearrange("p (g u) r -> p g r u", u=2)
             copy(eng, o[:, g0:g1, :, :], v[:, g0:g1, :, :])
 
         def quant(key, passes=(0, 1)):
-            if key not in codes:
-                codes[key] = work.tile([P, 2, P], U32, name="codes_" + key, tag="codes", bufs=8, align_bytes=64)
-                scl[key] = work.tile([P, 2, P], U8, name="scl_" + key, tag="scl", bufs=8, align_bytes=64)
+            t = place(grp, key, [2, P, 4], BF16, "grp", 3)
+            c = place(codes, key, [2, P], U32, "codes", 4)
+            s = place(scl, key, [2, P], U8, "scl", 4)
             g0, g1 = passes[0], passes[-1] + 1
             nc.vector.quantize_mx(
-                out=codes[key][:, g0:g1, :].rearrange("p g r -> p (g r)").bitcast(FP8X4),
-                scales=scl[key][:, g0:g1, :].rearrange("p g r -> p (g r)"),
-                in_=grp[key][:, g0:g1, :, :].rearrange("p g r t -> p (g r t)"),
+                out=c[:, g0:g1, :].rearrange("p g r -> p (g r)").bitcast(FP8X4),
+                scales=s[:, g0:g1, :].rearrange("p g r -> p (g r)"),
+                in_=t[:, g0:g1, :, :].rearrange("p g r t -> p (g r t)"),
+            )
+
+        def quant_xd(i):
+            place(codes, "x%d" % i, [2, P], U32, "codes", 4)
+            place(scl, "x%d" % i, [2, P], U8, "scl", 4)
+            k = "xd%d" % i
+            nc.vector.quantize_mx(
+                out=codes[k][:].rearrange("p a g r -> p (a g r)").bitcast(FP8X4),
+                scales=scl[k][:].rearrange("p a g r -> p (a g r)"),
+                in_=grp[k][:].rearrange("p a g r t -> p (a g r t)"),
             )
 
         def passes_into(t, key, w, h, passes=(0, 1)):
             for g in passes:
                 nc.tensor.matmul_mx(
                     out=t[:],
-                    lhsT=codes[key][:, g, :].bitcast(FP8X4),
-                    lhsT_scale=scl[key][:, g, :],
+                    lhsT=place(codes, key, [2, P], U32, "codes", 4)[:, g, :].bitcast(FP8X4),
+                    lhsT_scale=place(scl, key, [2, P], U8, "scl", 4)[:, g, :],
                     rhs=words[w, h][:, g, :].bitcast(FP4X4),
                     rhs_scale=planes[w][:, g, HALF * h : HALF * h + HALF],
                     start=(g == 0),
@@ -207,45 +223,42 @@ def tile_swigluforwardtangentjvp_d1p_kernel(
             nc.scalar.activation(out=t[:], in_=prod["g", j][:], func=func, scale=scale)
             val[name, j] = t
 
-        def fresh(name, j, dt=F32):
-            t = work.tile([P, HALF], dt, name="%s_%d" % (name, j), tag=name, align_bytes=64)
-            val[name, j] = t
-            return t
+        def half(name, j, dt=F32):
+            i, h = divmod(j, 2)
+            if (name, i) not in val:
+                val[name, i] = work.tile([P, 2, HALF], dt, name="%s_%d" % (name, i), tag=name, align_bytes=64)
+            return val[name, i][:, h, :]
 
         def m1(j):
-            t = fresh("m1", j)
             nc.vector.scalar_tensor_tensor(
-                out=t[:], in0=val["b", j][:], scalar=1.0, in1=prod["dg", j][:], op0=ALU.subtract, op1=ALU.mult
+                out=half("m1", j), in0=val["b", j][:], scalar=1.0, in1=prod["dg", j][:], op0=ALU.subtract, op1=ALU.mult
             )
 
         def m2(j):
-            t = fresh("m2", j)
             nc.vector.scalar_tensor_tensor(
-                out=t[:], in0=val["th", j][:], scalar=1.0, in1=prod["u", j][:], op0=ALU.add, op1=ALU.mult
+                out=half("m2", j), in0=val["th", j][:], scalar=1.0, in1=prod["u", j][:], op0=ALU.add, op1=ALU.mult
             )
 
         def m3(j):
-            t = fresh("m3", j)
             nc.vector.scalar_tensor_tensor(
-                out=t[:], in0=val["a", j][:], scalar=-2.0, in1=prod["du", j][:], op0=ALU.mult, op1=ALU.mult
+                out=half("m3", j), in0=val["a", j][:], scalar=-2.0, in1=prod["du", j][:], op0=ALU.mult, op1=ALU.mult
             )
 
-        def m4(j, eng="V"):
-            t = fresh("m4", j)
-            e = nc.vector if eng == "V" else nc.gpsimd
-            e.tensor_tensor(out=t[:], in0=val["m1", j][:], in1=val["m2", j][:], op=ALU.mult)
+        def m4(j):
+            nc.vector.tensor_tensor(out=half("m4", j), in0=half("m1", j), in1=half("m2", j), op=ALU.mult)
 
-        def dh(j, eng="V"):
-            if j < 0:
-                return
-            t = fresh("dh", j, BF16)
-            e = nc.vector if eng == "V" else nc.gpsimd
-            o, a, b = t[:], val["m3", j][:], val["m4", j][:]
-            if SPLIT_H:
-                o = o.rearrange("p (u q e) -> p q u e", u=2, e=2)
-                a = a.rearrange("p (q u e) -> p q u e", u=2, e=2)
-                b = b.rearrange("p (q u e) -> p q u e", u=2, e=2)
-            e.tensor_tensor(out=o, in0=a, in1=b, op=ALU.add)
+        def dh(j):
+            nc.vector.tensor_tensor(out=half("dh", j, BF16), in0=half("m3", j), in1=half("m4", j), op=ALU.add)
+
+        def whole(name, i, dt=F32):
+            half(name, 2 * i, dt)
+            return val[name, i][:]
+
+        def m4t(i, eng="V"):
+            (nc.vector if eng == "V" else nc.gpsimd).tensor_tensor(out=whole("m4", i), in0=whole("m1", i), in1=whole("m2", i), op=ALU.mult)
+
+        def dht(i):
+            nc.vector.tensor_tensor(out=whole("dh", i, BF16), in0=whole("m3", i), in1=whole("m4", i), op=ALU.add)
 
         def down(i, n, passes=(0, 1)):
             if ("o", i, n) not in prod:
@@ -272,168 +285,159 @@ def tile_swigluforwardtangentjvp_d1p_kernel(
 
         widen_half(0, 0, "V")
         turn_xp(0, 0)
+        widen_half(0, 1, "V")
         lift("x0", "V", (0,))
-        widen_half(0, 1, "S")
         quant("x0", (0,))
         turn_xp(0, 1)
-        turn_dxp(0, 0, "bank_u")
         turn_dxp(0, 1, "bank_du")
+        turn_dxp(0, 0, "bank_u")
         lift("x0", "S", (1,))
-        quant("x0", (1,))
-        lift("dx0", "V", (0,))
         lift("dx0", "V", (1,))
-        quant("dx0", (0,))
+        quant("x0", (1,))
+        lift("dx0", "S", (0,))
         quant("dx0", (1,))
-        widen_half(1, 1, "S")
+        quant("dx0", (0,))
         widen_half(1, 0, "V")
         product("g", 0)
         product("dg", 0)
-        turn_x(1)
-        turn_dx(1)
-        lift("x1", "V")
         act("b", 0)
-        act("th", 0)
-        product("g", 1)
-        act("a", 0)
-        quant("x1")
         product("u", 0)
-        lift("dx1", "S")
-        m1(0)
+        act("th", 0)
+        act("a", 0)
         product("du", 0)
-        product("dg", 1)
-        act("b", 1)
-        m2(0)
-        quant("dx1")
-        act("a", 1)
-        m3(0)
-        m1(1)
-        product("u", 1)
-        product("g", 2)
-        act("th", 1)
-        m4(0, "V")
-        product("du", 1)
+        turn_dx(1)
         widen_half(2, 0, "S")
+        widen_half(1, 1, "V")
+        turn_x(1)
+        m1(0)
+        product("g", 1)
+        m2(0)
+        lift("dx1", "S")
+        m3(0)
+        product("dg", 1)
+        lift("x1", "S")
+        product("u", 1)
+        product("du", 1)
+        act("b", 1)
+        act("th", 1)
+        quant_xd(1)
+        m1(1)
+        product("g", 2)
+        act("a", 1)
+        widen_half(2, 1, "S")
         m2(1)
         product("dg", 2)
-        widen_half(2, 1, "S")
         act("b", 2)
-        dh(0, "V")
-        m4(1, "V")
-        act("th", 2)
-        product("g", 3)
-        act("a", 2)
-        product("u", 2)
-        turn_x(2)
-        lift("x2", "S")
-        turn_dx(2)
         m3(1)
-        m1(2)
+        product("u", 2)
+        act("th", 2)
+        act("a", 2)
         product("du", 2)
-        product("dg", 3)
-        dh(1, "V")
-        act("b", 3)
-        m2(2)
-        quant("x2")
-        lift("dx2", "S")
-        turn_h(0)
-        act("a", 3)
-        m3(2)
-        m1(3)
-        product("u", 3)
-        product("g", 4)
-        act("th", 3)
-        quant("dx2")
-        lift("h0", "S")
-        m4(2, "V")
-        product("du", 3)
         widen_half(3, 0, "S")
+        turn_dx(2)
+        turn_x(2)
+        lift("dx2", "S")
+        m1(2)
+        m4t(0, "G")
+        product("g", 3)
+        m2(2)
+        lift("x2", "S")
+        m3(2)
+        product("dg", 3)
+        dht(0)
+        quant_xd(2)
+        product("u", 3)
+        product("du", 3)
+        act("b", 3)
+        act("th", 3)
+        m1(3)
+        product("g", 4)
+        act("a", 3)
+        widen_half(3, 1, "S")
         m2(3)
         product("dg", 4)
-        quant("h0")
-        widen_half(3, 1, "S")
         act("b", 4)
-        dh(2, "V")
-        m4(3, "V")
-        act("th", 4)
-        product("g", 5)
-        act("a", 4)
-        product("u", 4)
-        turn_x(3)
-        lift("x3", "S")
-        turn_dx(3)
         m3(3)
-        m1(4)
+        product("u", 4)
+        act("th", 4)
+        act("a", 4)
         product("du", 4)
-        product("dg", 5)
-        dh(3, "V")
-        act("b", 5)
-        m2(4)
-        quant("x3")
+        turn_dx(3)
+        turn_x(3)
         lift("dx3", "S")
-        turn_h(1)
-        act("a", 5)
+        m1(4)
+        m4t(1, "G")
+        turn_h(0)
+        product("g", 5)
+        m2(4)
+        lift("x3", "S")
         m3(4)
-        m1(5)
+        product("dg", 5)
+        lift("h0", "S")
+        dht(1)
+        quant_xd(3)
         product("u", 5)
-        product("g", 6)
-        act("th", 5)
-        down(0, 1)
-        quant("dx3")
-        lift("h1", "S")
-        m4(4, "V")
         product("du", 5)
+        quant("h0")
+        act("b", 5)
+        act("th", 5)
+        m1(5)
+        product("g", 6)
+        act("a", 5)
         m2(5)
         product("dg", 6)
-        quant("h1")
         act("b", 6)
-        dh(4, "V")
-        m4(5, "V")
-        act("th", 6)
-        product("g", 7)
-        act("a", 6)
-        product("u", 6)
         m3(5)
-        m1(6)
+        product("u", 6)
+        act("th", 6)
+        act("a", 6)
         product("du", 6)
-        product("dg", 7)
-        dh(5, "V")
-        act("b", 7)
+        m1(6)
+        m4t(2, "G")
+        turn_h(1)
+        product("g", 7)
         m2(6)
-        turn_h(2)
-        act("a", 7)
         m3(6)
-        m1(7)
+        product("dg", 7)
+        lift("h1", "S")
+        dht(2)
         product("u", 7)
-        act("th", 7)
-        down(1, 1)
-        lift("h2", "S")
         product("du", 7)
-        m4(6, "V")
+        quant("h1")
+        act("b", 7)
+        act("th", 7)
+        m1(7)
+        act("a", 7)
         m2(7)
-        quant("h2")
-        m4(7, "V")
-        store(0, 1, "S")
         m3(7)
-        down(0, 0)
-        down(2, 1)
-        dh(6, "V")
+        turn_h(2)
+        lift("h2", "S")
+        quant("h2")
+        down(0, 1)
+        store(0, 1, "S")
+        down(1, 1)
         store(1, 1, "S")
-        dh(7, "V")
+        down(2, 1)
+        down(0, 0)
+        store(2, 1, "S")
         store(0, 0, "S")
+        m4(6)
+        m4(7)
+        dh(6)
+        dh(7)
         down(1, 0)
         turn_h(3, (0,))
-        store(2, 1, "S")
-        store(1, 0, "S")
         turn_h(3, (1,))
-        lift("h3", "S", (0,))
+        store(1, 0, "S")
         down(2, 0)
+        lift("h3", "S", (0,))
         lift("h3", "S", (1,))
         store(2, 0, "S")
         quant("h3", (0,))
-        down(3, 0, (0,))
         quant("h3", (1,))
-        down(3, 1, (0,))
+        down(3, 0, (0,))
         down(3, 0, (1,))
+        down(3, 1, (0,))
         down(3, 1, (1,))
         store(3, 0, "S")
         store(3, 1, "V")

from contextlib import ExitStack

import concourse.mybir as mybir
from concourse.masks import make_identity

N, D, F = 512, 1024, 1024
FLOPS = 5 * 2 * N * D * F

P = 128
TILES = N // P
HALF = 512
UNITS = 2 * TILES
SPLIT_H = False

F32 = mybir.dt.float32
BF16 = mybir.dt.bfloat16
I32 = mybir.dt.int32
U32 = mybir.dt.uint32
U8 = mybir.dt.uint8
E4M3 = mybir.dt.float8_e4m3fn
FP8X4 = mybir.dt.float8_e4m3fn_x4
FP4X4 = mybir.dt.float4_e2m1fn_x4
ALU = mybir.AluOpType
ACT = mybir.ActivationFunctionType


def tile_swigluforwardtangentjvp_d1p_kernel(
    tc, x_bytes, x_scale, dx, wg_words, wg_scales, wu_words, wu_scales, wd_words, wd_scales, out
):
    nc = tc.nc
    xb_v = x_bytes.rearrange("(p i) k -> p i k", i=TILES)
    xs_v = x_scale.rearrange("(p i) j -> p i j", i=TILES)
    dx_v = dx.rearrange("(p i) k -> p i k", i=TILES)
    out_v = out.rearrange("(p i) d -> p i d", i=TILES)

    with ExitStack() as ctx:
        keep = ctx.enter_context(tc.tile_pool(name="keep", bufs=1))
        work = ctx.enter_context(tc.tile_pool(name="work", bufs=3))
        psum = ctx.enter_context(tc.psum_pool(name="psum", bufs=1))
        ctx.enter_context(tc.manual_schedule())

        ident = keep.tile([P, P], F32, name="ident")
        xs = keep.tile([P, TILES, 8], F32, name="xs")
        xb = keep.tile([P, TILES, D], U8, name="xb", align_bytes=64)
        dxt = keep.tile([P, TILES, D], BF16, name="dxt", align_bytes=64)
        one = keep.tile([P, 1], F32, name="one")
        one_o = keep.tile([P, 1], F32, name="one_o")
        words = {}
        planes = {}
        hbm = {"g": (wg_words, wg_scales), "u": (wu_words, wu_scales), "d": (wd_words, wd_scales)}
        for w in "gud":
            for h in range(2):
                words[w, h] = keep.tile([P, 2, 1024], U8, name="words_%s%d" % (w, h), align_bytes=64)
            planes[w] = keep.tile([P, 2, 1024], U8, name="plane_" + w, align_bytes=64)

        def load_words(w, h):
            nc.sync.dma_start(
                out=words[w, h][:].bitcast(I32),
                in_=hbm[w][0].bitcast(I32).rearrange("g p c -> p g c")[:, :, 256 * h : 256 * h + 256],
            )

        def load_scales(w, queue, quadrants=range(4)):
            src = hbm[w][1].bitcast(I32)
            dst = planes[w][:].bitcast(I32)
            for q in quadrants:
                queue.dma_start(
                    out=dst[32 * q : 32 * q + 4, :, :],
                    in_=src[:, 4 * q : 4 * q + 4, :].rearrange("g r n -> r g n"),
                )

        def load_x(i):
            nc.sync.dma_start(out=xb[:, i, :], in_=xb_v[:, i, :])

        def load_dx(i):
            nc.sync.dma_start(out=dxt[:, i, :], in_=dx_v[:, i, :])

        nc.vector.memset(planes["g"][:].bitcast(I32), 0)
        nc.vector.memset(one[:], 1.0)
        nc.vector.memset(planes["u"][:].bitcast(I32), 0)
        nc.vector.memset(planes["d"][:].bitcast(I32), 0)
        make_identity(nc, ident[:])
        nc.scalar.dma_start(out=xs[:], in_=xs_v)
        load_x(0)
        load_dx(0)
        load_scales("g", nc.sync)
        nc.scalar.activation(out=one_o[:], in_=one[:], func=ACT.Silu)
        load_words("g", 0)
        load_scales("u", nc.sync)
        load_words("u", 0)
        nc.sync.dma_start(out=xb[:, 1:4, :], in_=xb_v[:, 1:4, :])
        load_dx(1)
        load_words("g", 1)
        load_words("u", 1)
        nc.sync.dma_start(out=dxt[:, 2:4, :], in_=dx_v[:, 2:4, :])
        load_words("d", 0)
        load_words("d", 1)
        load_scales("d", nc.sync)

        xw = {}
        bank = {}
        grp = {}
        codes = {}
        scl = {}
        val = {}
        prod = {}

        def widen(i, engines):
            xw[i] = work.tile([P, D], BF16, name="xw%d" % i, tag="xw", align_bytes=64)
            for b in range(8):
                o = xw[i][:, 128 * b : 128 * b + 128]
                v = xb[:, i, 128 * b : 128 * b + 128].bitcast(E4M3)
                s = xs[:, i, b : b + 1]
                if engines[b] == "V":
                    nc.vector.tensor_scalar(out=o, in0=v, scalar1=s, scalar2=None, op0=ALU.mult)
                else:
                    nc.scalar.activation(out=o, in_=v, func=ACT.Copy, scale=s)

        def widen_half(i, g, eng):
            if i not in xw:
                xw[i] = work.tile([P, D], BF16, name="xw%d" % i, tag="xw", align_bytes=64)
            for b in range(4 * g, 4 * g + 4):
                o = xw[i][:, 128 * b : 128 * b + 128]
                v = xb[:, i, 128 * b : 128 * b + 128].bitcast(E4M3)
                s = xs[:, i, b : b + 1]
                if eng == "V":
                    nc.vector.tensor_scalar(out=o, in0=v, scalar1=s, scalar2=None, op0=ALU.mult)
                else:
                    nc.scalar.activation(out=o, in_=v, func=ACT.Copy, scale=s)

        def turn_xp(i, g, tag="aux"):
            turn("x%d" % i, [(g, xw[i][:, 512 * g : 512 * g + 512])], tag)

        def turn_dxp(i, g, tag="aux"):
            turn("dx%d" % i, [(g, dxt[:, i, 512 * g : 512 * g + 512])], tag)

        def copy(eng, out, in_):
            if eng == "V":
                nc.vector.tensor_copy(out=out, in_=in_)
            else:
                nc.scalar.copy(out=out, in_=in_)

        def turn(key, parts, tag="aux"):
            t = psum.tile([P, 4, P], F32, name="turn_%s_%d" % (key, parts[0][0]), tag=tag, bufs=3 if tag == "aux" else 1)
            for g, part in parts:
                w = part.bitcast(F32)
                for u in range(2):
                    cols = slice(128 * u, 128 * u + 128) if SPLIT_H and key[0] == "h" else slice(u, 256, 2)
                    nc.tensor.transpose(t[:, 2 * g + u, :], w[:, cols], ident[:])
                bank[key, g] = t

        def turn_x(i):
            turn("x%d" % i, [(g, xw[i][:, 512 * g : 512 * g + 512]) for g in range(2)])

        def turn_dx(i):
            turn("dx%d" % i, [(g, dxt[:, i, 512 * g : 512 * g + 512]) for g in range(2)])

        def turn_h(i, halves=(0, 1)):
            turn("h%d" % i, [(g, half("dh", 2 * i + g, BF16)) for g in halves])

        def place(store, key, shape, dtype, tag, bufs):
            if key[0] == "h":
                if key not in store:
                    store[key] = work.tile([P] + shape, dtype, name=tag + key, tag=tag + "h", bufs=bufs, align_bytes=64)
                return store[key][:]
            i = key[-1]
            if "xd" + i not in store:
                store["xd" + i] = work.tile([P, 2] + shape, dtype, name=tag + "xd" + i, tag=tag, bufs=bufs, align_bytes=64)
            return store["xd" + i][:, 1 if key[0] == "d" else 0]

        def lift(key, eng, passes=(0, 1)):
            t = place(grp, key, [2, P, 4], BF16, "grp", 3)
            g0, g1 = passes[0], passes[-1] + 1
            o = t.rearrange("p g r t -> p (g r t)").bitcast(F32).rearrange("p (g r u) -> p g r u", g=2, u=2)
            v = bank[key, g0][:].rearrange("p (g u) r -> p g r u", u=2)
            copy(eng, o[:, g0:g1, :, :], v[:, g0:g1, :, :])

        def quant(key, passes=(0, 1)):
            t = place(grp, key, [2, P, 4], BF16, "grp", 3)
            c = place(codes, key, [2, P], U32, "codes", 4)
            s = place(scl, key, [2, P], U8, "scl", 4)
            g0, g1 = passes[0], passes[-1] + 1
            nc.vector.quantize_mx(
                out=c[:, g0:g1, :].rearrange("p g r -> p (g r)").bitcast(FP8X4),
                scales=s[:, g0:g1, :].rearrange("p g r -> p (g r)"),
                in_=t[:, g0:g1, :, :].rearrange("p g r t -> p (g r t)"),
            )

        def quant_xd(i):
            place(codes, "x%d" % i, [2, P], U32, "codes", 4)
            place(scl, "x%d" % i, [2, P], U8, "scl", 4)
            k = "xd%d" % i
            nc.vector.quantize_mx(
                out=codes[k][:].rearrange("p a g r -> p (a g r)").bitcast(FP8X4),
                scales=scl[k][:].rearrange("p a g r -> p (a g r)"),
                in_=grp[k][:].rearrange("p a g r t -> p (a g r t)"),
            )

        def passes_into(t, key, w, h, passes=(0, 1)):
            for g in passes:
                nc.tensor.matmul_mx(
                    out=t[:],
                    lhsT=place(codes, key, [2, P], U32, "codes", 4)[:, g, :].bitcast(FP8X4),
                    lhsT_scale=place(scl, key, [2, P], U8, "scl", 4)[:, g, :],
                    rhs=words[w, h][:, g, :].bitcast(FP4X4),
                    rhs_scale=planes[w][:, g, HALF * h : HALF * h + HALF],
                    start=(g == 0),
                    stop=(g == 1),
                )

        def product(kind, j):
            if j >= UNITS:
                return
            i, h = divmod(j, 2)
            t = psum.tile([P, HALF], F32, name="%s_%d" % (kind, j), tag="bank_" + kind, bufs=2 if kind == "g" else 1)
            passes_into(t, ("dx%d" if kind[0] == "d" else "x%d") % i, kind[-1], h)
            prod[kind, j] = t

        def act(name, j):
            if j >= UNITS:
                return
            func, scale = {"b": (ACT.Silu, -1.0), "th": (ACT.Tanh, 0.5), "a": (ACT.Silu, 1.0)}[name]
            t = work.tile([P, HALF], F32, name="%s_%d" % (name, j), tag=name)
            nc.scalar.activation(out=t[:], in_=prod["g", j][:], func=func, scale=scale)
            val[name, j] = t

        def half(name, j, dt=F32):
            i, h = divmod(j, 2)
            if (name, i) not in val:
                val[name, i] = work.tile([P, 2, HALF], dt, name="%s_%d" % (name, i), tag=name, align_bytes=64)
            return val[name, i][:, h, :]

        def m1(j):
            nc.vector.scalar_tensor_tensor(
                out=half("m1", j), in0=val["b", j][:], scalar=1.0, in1=prod["dg", j][:], op0=ALU.subtract, op1=ALU.mult
            )

        def m2(j):
            nc.vector.scalar_tensor_tensor(
                out=half("m2", j), in0=val["th", j][:], scalar=1.0, in1=prod["u", j][:], op0=ALU.add, op1=ALU.mult
            )

        def m3(j):
            nc.vector.scalar_tensor_tensor(
                out=half("m3", j), in0=val["a", j][:], scalar=-2.0, in1=prod["du", j][:], op0=ALU.mult, op1=ALU.mult
            )

        def m4(j):
            nc.vector.tensor_tensor(out=half("m4", j), in0=half("m1", j), in1=half("m2", j), op=ALU.mult)

        def dh(j):
            nc.vector.tensor_tensor(out=half("dh", j, BF16), in0=half("m3", j), in1=half("m4", j), op=ALU.add)

        def whole(name, i, dt=F32):
            half(name, 2 * i, dt)
            return val[name, i][:]

        def m4t(i, eng="V"):
            (nc.vector if eng == "V" else nc.gpsimd).tensor_tensor(out=whole("m4", i), in0=whole("m1", i), in1=whole("m2", i), op=ALU.mult)

        def dht(i):
            nc.vector.tensor_tensor(out=whole("dh", i, BF16), in0=whole("m3", i), in1=whole("m4", i), op=ALU.add)

        def down(i, n, passes=(0, 1)):
            if ("o", i, n) not in prod:
                prod["o", i, n] = psum.tile([P, HALF], F32, name="down_%d_%d" % (i, n), tag="aux", bufs=3)
            passes_into(prod["o", i, n], "h%d" % i, "d", n, passes)

        def store_half(i, n, c, eng):
            t = work.tile([P, 256], F32, name="out_%d_%d_%d" % (i, n, c), tag="outh", bufs=4)
            src = prod["o", i, n][:, 256 * c : 256 * c + 256]
            if eng == "V":
                nc.vector.tensor_scalar(out=t[:], in0=src, scalar1=-0.5, scalar2=None, op0=ALU.mult)
            else:
                nc.scalar.activation(out=t[:], in_=src, func=ACT.Copy, scale=-0.5)
            lo = HALF * n + 256 * c
            (nc.sync if eng == "V" else nc.scalar).dma_start(out=out_v[:, i, lo : lo + 256], in_=t[:])

        def store(i, n, eng, queue=None):
            t = work.tile([P, HALF], F32, name="out_%d_%d" % (i, n), tag="out", bufs=8)
            if eng == "V":
                nc.vector.tensor_scalar(out=t[:], in0=prod["o", i, n][:], scalar1=-0.5, scalar2=None, op0=ALU.mult)
            else:
                nc.scalar.activation(out=t[:], in_=prod["o", i, n][:], func=ACT.Copy, scale=-0.5)
            (queue or nc.sync).dma_start(out=out_v[:, i, HALF * n : HALF * n + HALF], in_=t[:])

        widen_half(0, 0, "V")
        turn_xp(0, 0)
        widen_half(0, 1, "V")
        lift("x0", "V", (0,))
        quant("x0", (0,))
        turn_xp(0, 1)
        turn_dxp(0, 1, "bank_du")
        turn_dxp(0, 0, "bank_u")
        lift("x0", "S", (1,))
        lift("dx0", "V", (1,))
        quant("x0", (1,))
        lift("dx0", "S", (0,))
        quant("dx0", (1,))
        quant("dx0", (0,))
        widen_half(1, 0, "V")
        product("g", 0)
        product("dg", 0)
        act("b", 0)
        product("u", 0)
        act("th", 0)
        act("a", 0)
        product("du", 0)
        turn_dx(1)
        widen_half(2, 0, "S")
        widen_half(1, 1, "V")
        turn_x(1)
        m1(0)
        product("g", 1)
        m2(0)
        lift("dx1", "S")
        m3(0)
        product("dg", 1)
        lift("x1", "S")
        product("u", 1)
        product("du", 1)
        act("b", 1)
        act("th", 1)
        quant_xd(1)
        m1(1)
        product("g", 2)
        act("a", 1)
        widen_half(2, 1, "S")
        m2(1)
        product("dg", 2)
        act("b", 2)
        m3(1)
        product("u", 2)
        act("th", 2)
        act("a", 2)
        product("du", 2)
        widen_half(3, 0, "S")
        turn_dx(2)
        turn_x(2)
        lift("dx2", "S")
        m1(2)
        m4t(0, "G")
        product("g", 3)
        m2(2)
        lift("x2", "S")
        m3(2)
        product("dg", 3)
        dht(0)
        quant_xd(2)
        product("u", 3)
        product("du", 3)
        act("b", 3)
        act("th", 3)
        m1(3)
        product("g", 4)
        act("a", 3)
        widen_half(3, 1, "S")
        m2(3)
        product("dg", 4)
        act("b", 4)
        m3(3)
        product("u", 4)
        act("th", 4)
        act("a", 4)
        product("du", 4)
        turn_dx(3)
        turn_x(3)
        lift("dx3", "S")
        m1(4)
        m4t(1, "G")
        turn_h(0)
        product("g", 5)
        m2(4)
        lift("x3", "S")
        m3(4)
        product("dg", 5)
        lift("h0", "S")
        dht(1)
        quant_xd(3)
        product("u", 5)
        product("du", 5)
        quant("h0")
        act("b", 5)
        act("th", 5)
        m1(5)
        product("g", 6)
        act("a", 5)
        m2(5)
        product("dg", 6)
        act("b", 6)
        m3(5)
        product("u", 6)
        act("th", 6)
        act("a", 6)
        product("du", 6)
        m1(6)
        m4t(2, "G")
        turn_h(1)
        product("g", 7)
        m2(6)
        m3(6)
        product("dg", 7)
        lift("h1", "S")
        dht(2)
        product("u", 7)
        product("du", 7)
        quant("h1")
        act("b", 7)
        act("th", 7)
        m1(7)
        act("a", 7)
        m2(7)
        m3(7)
        turn_h(2)
        lift("h2", "S")
        quant("h2")
        down(0, 1)
        store(0, 1, "S")
        down(1, 1)
        store(1, 1, "S")
        down(2, 1)
        down(0, 0)
        store(2, 1, "S")
        store(0, 0, "S")
        m4(6)
        m4(7)
        dh(6)
        dh(7)
        down(1, 0)
        turn_h(3, (0,))
        turn_h(3, (1,))
        store(1, 0, "S")
        down(2, 0)
        lift("h3", "S", (0,))
        lift("h3", "S", (1,))
        store(2, 0, "S")
        quant("h3", (0,))
        quant("h3", (1,))
        down(3, 0, (0,))
        down(3, 0, (1,))
        down(3, 1, (0,))
        down(3, 1, (1,))
        store(3, 0, "S")
        store(3, 1, "V")
